import numpy as np
import ml_dtypes


def mxq(x, axis, fmt="e4m3"):
    dtype, down = {"e4m3": (ml_dtypes.float8_e4m3fn, 7), "e5m2": (ml_dtypes.float8_e5m2, 14)}[fmt]
    v = np.moveaxis(np.asarray(x, np.float32).astype(ml_dtypes.bfloat16).astype(np.float64), axis, -1)
    blocks = v.reshape(v.shape[:-1] + (-1, 32))
    amax = np.abs(blocks).max(-1, keepdims=True)
    byte = np.maximum(np.where(amax > 0, np.frexp(amax)[1] - 1 + 127, 0) - down, 1)
    scale = np.exp2(byte - 127.0)
    codes = (blocks / scale).astype(np.float32).astype(dtype).astype(np.float64)
    return np.moveaxis((codes * scale).reshape(v.shape), -1, axis)


WIDE = False


def mx_kscale(k):
    if not WIDE:
        return np.ones(k)
    levels = np.array([10, -10, 5, -5, 0])
    if k % 512:
        return np.exp2(np.random.permutation(np.resize(levels, k // 32))).repeat(32)
    a = np.empty((k // 512, 16))
    for p in range(k // 512):
        a[p, :8] = np.random.permutation(np.resize(levels, 8))
        for g in range(8):
            far = levels[np.abs(levels - a[p, g]) >= 10]
            a[p, g + 8] = far[np.random.randint(len(far))]
    return np.exp2(a.ravel()).repeat(32)


def f64(x):
    return np.asarray(x).astype(np.float64)


def striped(idx):
    return np.tile(np.asarray(idx).reshape(-1, 16).T, (8, 1)).astype(np.uint16)


def unstriped(offs):
    return offs[:16].T.reshape(-1).astype(np.int64)


E2M1 = np.array([0.0, 0.5, 1.0, 1.5, 2.0, 3.0, 4.0, 6.0, -0.0, -0.5, -1.0, -1.5, -2.0, -3.0, -4.0, -6.0])


def pack_weight(w, fmt):
    k, n = w.shape
    w = f64(np.asarray(w, np.float32).astype(ml_dtypes.bfloat16)).reshape(k // 32, 32, n)
    amax = np.abs(w).max(1)
    if fmt == "e4m3":
        byte = np.frexp(amax)[1] - 1 + 127 - 7
    else:
        mant, ex = np.frexp(amax / 6.0)
        byte = np.where(mant > 0.5, ex, ex - 1) + 127
    byte = np.clip(np.where(amax > 0, byte, 1), 1, 254)
    scaled = (w * np.exp2(127.0 - byte)[:, None, :]).reshape(k, n).astype(np.float32)
    by_word = np.ascontiguousarray(scaled.reshape(k // 512, 128, 4, n).transpose(0, 1, 3, 2))
    if fmt == "e4m3":
        words = by_word.astype(ml_dtypes.float8_e4m3fn).view(np.uint8)
    else:
        c = by_word.astype(ml_dtypes.float4_e2m1fn).view(np.uint8) & 0xF
        words = (c[..., 0::2] | (c[..., 1::2] << 4)).reshape(k // 512, 128, 2 * n)
    return np.ascontiguousarray(words), np.ascontiguousarray(byte.astype(np.uint8).reshape(k // 512, 16, n))


def unpack_weight(words, scales, fmt):
    g, _, n = scales.shape
    words = np.ascontiguousarray(words).reshape(g, 128, n, -1)
    if fmt == "e4m3":
        vals = words.view(ml_dtypes.float8_e4m3fn).astype(np.float64)
    else:
        nib = np.empty((g, 128, n, 4), np.uint8)
        nib[..., 0::2] = words & 0xF
        nib[..., 1::2] = words >> 4
        vals = E2M1[nib]
    vals = vals * np.repeat(np.exp2(scales.astype(np.float64) - 127.0), 8, axis=1)[..., None]
    return vals.transpose(0, 1, 3, 2).reshape(g * 512, n)


def softplus(v):
    return np.log(1.0 + np.exp(v))


def sigmoid(v):
    return 1.0 / (1.0 + np.exp(-v))


D, E, T, I, Q, G = 512, 512, 2048, 512, 128, 64


def setup_inputs():
    n = np.random.standard_normal
    idx = np.random.permutation(T)[:I]
    fd = mx_kscale(D)
    fe = mx_kscale(E)
    keysp = pack_weight(n((D, T)) / fd[:, None], "e2m1")
    valsp = pack_weight(n((E, T)) / fe[:, None], "e2m1")
    return {
        "query": (n((D, Q)) * 0.8 / np.sqrt(D) * fd[:, None]).astype(np.float32),
        "query2": (n((D, Q)) * 1.0 / np.sqrt(D) * fd[:, None]).astype(np.float32),
        "keys_words": keysp[0],
        "keys_scales": keysp[1],
        "reserve": (np.random.uniform(2.0, 10.0, (Q, 1))).astype(np.float32),
        "gout": (n((E, Q)) * 1 / np.sqrt(E) * fe[:, None]).astype(np.float32),
        "vals_words": valsp[0],
        "vals_scales": valsp[1],
        "base": (0.5 * n((Q, I))).astype(np.float32),
        "offs": striped(idx),
    }


def reference(query, query2, keys_words, keys_scales, reserve, gout, vals_words, vals_scales, base, offs):
    idx = unstriped(offs)
    keysu = unpack_weight(keys_words, keys_scales, "e2m1")
    valsu = unpack_weight(vals_words, vals_scales, "e2m1")
    queryq = mxq(f64(query), 0, "e4m3")
    keysidxg = keysu[:, idx]
    a = queryq.T @ keysidxg
    query2q = mxq(f64(query2), 0, "e4m3")
    b = query2q.T @ keysidxg
    m1 = b.reshape(Q, G, I // G).mean(axis=2)
    q0 = softplus(m1 * 3.0)
    z = np.sum(q0, axis=1, keepdims=True) + f64(reserve)
    pa = np.exp(a)
    s = pa.reshape(Q, G, I // G).sum(axis=2)
    goutq = mxq(f64(gout), 0, "e4m3")
    valsidxg = valsu[:, idx]
    c0 = goutq.T @ valsidxg
    drr = c0 * pa
    dr = drr.reshape(Q, G, I // G).sum(axis=2)
    dz = np.sum(dr * q0 / s / np.square(z) * (-1.0), axis=1, keepdims=True)
    dq0 = dr / z / s + dz
    dm1 = dq0 * sigmoid(m1 * 3.0) * 3.0
    e1 = dm1 / 8.0
    r1 = np.repeat(e1, I // G, axis=1)
    hr1 = r1 * 1024.0 * 2.0 * 1024.0
    he1 = hr1.reshape(Q, G, I // G).sum(axis=2)
    hdm1 = he1 / 8.0
    hdq0 = hdm1 * 3.0 * sigmoid(m1 * 3.0)
    hdz = np.sum(hdq0, axis=1, keepdims=True)
    hz = np.sum(hdq0 / s * dr / np.square(z) * (-1.0), axis=1, keepdims=True) + np.sum(hdz * (-1.0) * dr * q0 / s / np.square(np.square(z)) * (-1.0), axis=1, keepdims=True) * z * 2.0
    hq0 = hdz * (-1.0) / np.square(z) * dr / s + hz
    hm1 = hdm1 * 3.0 * dq0 * sigmoid(m1 * 3.0) * (1.0 - sigmoid(m1 * 3.0)) * 3.0 + hq0 * sigmoid(m1 * 3.0) * 3.0
    e51 = hm1 / 8.0
    r51 = np.repeat(e51, I // G, axis=1)
    y = r51 + f64(base)
    return y

@@ -1,0 +1,188 @@
+from contextlib import ExitStack
+
+import concourse.mybir as mybir
+
+F32 = mybir.dt.float32
+BF16 = mybir.dt.bfloat16
+I32 = mybir.dt.int32
+U32 = mybir.dt.uint32
+U16 = mybir.dt.uint16
+U8 = mybir.dt.uint8
+FP8X4 = mybir.dt.float8_e4m3fn_x4
+FP4X4 = mybir.dt.float4_e2m1fn_x4
+ALU = mybir.AluOpType
+ACT = mybir.ActivationFunctionType
+AX = mybir.AxisListType
+
+P = 128
+PACK = 4
+TOKENS = 2048
+SLOTS = 512
+ROWS = 128
+PAGES = 64
+PAGE = 8
+FLOPS = 3 * 2 * 512 * ROWS * SLOTS
+GAIN = 9.0 * 3.0 * 1024.0 * 2.0 * 1024.0 / 64.0
+
+
+def tile_attend_gppagequotas_kernel(tc, query, query2, keys_words, keys_scales, reserve, gout, vals_words, vals_scales, base, offs, out):
+    nc = tc.nc
+    with ExitStack() as ctx:
+        sb = ctx.enter_context(tc.tile_pool(name="sb", bufs=1))
+        ps = ctx.enter_context(tc.psum_pool(name="ps", bufs=1))
+
+        offsets = sb.tile([P, SLOTS // 16], U16, name="offsets")
+        k_words = sb.tile([P, TOKENS], U16, name="k_words", align_bytes=64)
+        k_bytes = sb.tile([P, TOKENS], U8, name="k_bytes", align_bytes=64)
+        v_bytes = sb.tile([P, TOKENS], U8, name="v_bytes", align_bytes=64)
+        q_raw = sb.tile([P, PACK, ROWS], F32, name="q_raw")
+        q2_raw = sb.tile([P, PACK, ROWS], F32, name="q2_raw", tag="q2_then_v", align_bytes=64)
+        g_raw = sb.tile([P, PACK, ROWS], F32, name="g_raw", tag="g_then_pa")
+        base_sb = sb.tile([P, PAGES, PAGE], F32, name="base_sb")
+        reserve_sb = sb.tile([P, 1], F32, name="reserve_sb")
+
+        def load_scale_rows(plane, rows):
+            by_place = rows[0].rearrange("(q r) c -> r q c", r=4)
+            for r in range(4):
+                nc.sync.dma_start(out=plane[r:P:32, :].bitcast(I32), in_=by_place[r].bitcast(I32))
+
+        def load_rows(queue, raw, src):
+            queue.dma_start(out=raw[:], in_=src.rearrange("(p j) w -> p j w", j=PACK))
+
+        nc.vector.memset(k_bytes[:].bitcast(I32), 0)
+        nc.gpsimd.memset(v_bytes[:].bitcast(I32), 0)
+        nc.sync.dma_start(offsets[:], offs)
+        nc.scalar.dma_start(out=k_words[:].bitcast(I32), in_=keys_words[0].bitcast(I32))
+        load_rows(nc.scalar, q2_raw, query2)
+        load_scale_rows(k_bytes, keys_scales)
+        load_scale_rows(v_bytes, vals_scales)
+        load_rows(nc.gpsimd, q_raw, query)
+        load_rows(nc.gpsimd, g_raw, gout)
+        nc.gpsimd.dma_start(out=reserve_sb[:], in_=reserve)
+        nc.gpsimd.dma_start(out=base_sb[:].rearrange("p g j -> p (g j)"), in_=base)
+
+        kg_bytes = sb.tile([P, SLOTS], U8, name="kg_bytes", align_bytes=64)
+        kg_words = sb.tile([P, SLOTS], U16, name="kg_words", align_bytes=64)
+        vg_bytes = sb.tile([P, SLOTS], U8, name="vg_bytes", align_bytes=64)
+        vg_words = sb.tile([P, SLOTS], U16, name="vg_words", align_bytes=64)
+        qq_bf = sb.tile([P, 2, ROWS, PACK], BF16, name="qq_bf", align_bytes=64)
+        g_bf = sb.tile([P, ROWS, PACK], BF16, name="g_bf", align_bytes=64)
+        qq_codes = sb.tile([P, 2 * ROWS], U32, name="qq_codes", align_bytes=64)
+        qq_bytes = sb.tile([P, 2 * ROWS], U8, name="qq_bytes", align_bytes=64)
+        g_codes = sb.tile([P, ROWS], U32, name="g_codes", align_bytes=64)
+        g_bytes = sb.tile([P, ROWS], U8, name="g_bytes", align_bytes=64)
+
+        nc.scalar.copy(out=qq_bf[:, 0], in_=q2_raw[:].rearrange("p j w -> p w j"))
+        v_words = sb.tile([P, TOKENS], U16, name="v_words", tag="q2_then_v", align_bytes=64)
+        nc.sync.dma_start(out=v_words[:].bitcast(I32), in_=vals_words[0].bitcast(I32))
+        nc.scalar.copy(out=qq_bf[:, 1], in_=q_raw[:].rearrange("p j w -> p w j"))
+        nc.scalar.copy(out=g_bf[:], in_=g_raw[:].rearrange("p j w -> p w j"))
+
+        nc.vector.tensor_copy(kg_bytes[:], k_bytes[:].indirect(offsets[:]))
+        nc.vector.tensor_copy(kg_words[:], k_words[:].indirect(offsets[:]))
+        nc.vector.quantize_mx(out=qq_codes[:].bitcast(FP8X4), scales=qq_bytes[:], in_=qq_bf[:].rearrange("p s w j -> p (s w j)"))
+
+        b_ps = ps.tile([P, PAGES, PAGE], F32, name="b_ps")
+        a_ps = ps.tile([P, PAGES, PAGE], F32, name="a_ps")
+        c_ps = ps.tile([P, PAGES, PAGE], F32, name="c_ps")
+
+        def product(acc, codes, scale_bytes, words, word_bytes):
+            nc.tensor.matmul_mx(
+                out=acc[:].rearrange("p g j -> p (g j)"),
+                lhsT=codes.bitcast(FP8X4),
+                lhsT_scale=scale_bytes,
+                rhs=words[:].bitcast(FP4X4),
+                rhs_scale=word_bytes[:],
+                start=True,
+                stop=True,
+            )
+
+        product(b_ps, qq_codes[:, 0:ROWS], qq_bytes[:, 0:ROWS], kg_words, kg_bytes)
+        product(a_ps, qq_codes[:, ROWS:], qq_bytes[:, ROWS:], kg_words, kg_bytes)
+
+        nc.vector.tensor_copy(vg_bytes[:], v_bytes[:].indirect(offsets[:]))
+
+        def small(name):
+            return sb.tile([P, PAGES], F32, name=name)
+
+        def column(name):
+            return sb.tile([P, 1], F32, name=name)
+
+        b_sum = small("b_sum")
+        nc.vector.tensor_reduce(out=b_sum[:], in_=b_ps[:], axis=AX.X, op=ALU.add)
+
+        pa = sb.tile([P, PAGES, PAGE], F32, name="pa", tag="g_then_pa")
+        nc.scalar.activation(out=pa[:], in_=a_ps[:], func=ACT.Exp)
+        x_abs = small("x_abs")
+        nc.scalar.activation(out=x_abs[:], in_=b_sum[:], func=ACT.Abs, scale=3.0 / PAGE)
+        x_pos = small("x_pos")
+        x_pos_sum = column("x_pos_sum")
+        nc.scalar.activation(out=x_pos[:], in_=b_sum[:], func=ACT.Relu, scale=3.0 / PAGE, accum_out=x_pos_sum[:])
+        half_tanh = small("half_tanh")
+        nc.scalar.activation(out=half_tanh[:], in_=b_sum[:], func=ACT.Tanh, scale=1.5 / PAGE)
+        decay = small("decay")
+        nc.scalar.activation(out=decay[:], in_=x_abs[:], func=ACT.Exp, scale=-1.0)
+        log_term = small("log_term")
+        log_sum = column("log_sum")
+        nc.scalar.activation(out=log_term[:], in_=decay[:], func=ACT.Ln, bias=1.0, accum_out=log_sum[:])
+        z_part = column("z_part")
+        nc.scalar.activation(out=z_part[:], in_=x_pos_sum[:], func=ACT.Identity, bias=reserve_sb[:])
+        z = column("z")
+        nc.scalar.activation(out=z[:], in_=log_sum[:], func=ACT.Identity, bias=z_part[:])
+        sig = small("sig")
+        nc.scalar.activation(out=sig[:], in_=half_tanh[:], func=ACT.Copy, scale=0.5, bias=0.5)
+        sig_neg = small("sig_neg")
+        nc.scalar.activation(out=sig_neg[:], in_=half_tanh[:], func=ACT.Copy, scale=-0.5, bias=-0.5)
+        sig_rest = small("sig_rest")
+        nc.scalar.activation(out=sig_rest[:], in_=half_tanh[:], func=ACT.Copy, scale=-0.5, bias=0.5)
+
+        nc.vector.tensor_copy(vg_words[:], v_words[:].indirect(offsets[:]))
+        nc.vector.quantize_mx(out=g_codes[:].bitcast(FP8X4), scales=g_bytes[:], in_=g_bf[:].rearrange("p w j -> p (w j)"))
+        product(c_ps, g_codes[:], g_bytes[:], vg_words, vg_bytes)
+
+        s = small("s")
+        nc.vector.tensor_reduce(out=s[:], in_=pa[:], axis=AX.X, op=ALU.add)
+        s_inv = small("s_inv")
+        nc.vector.reciprocal(out=s_inv[:], in_=s[:])
+        drr = sb.tile([P, PAGES, PAGE], F32, name="drr")
+        nc.vector.tensor_tensor(out=drr[:], in0=c_ps[:], in1=pa[:], op=ALU.mult)
+        q0 = small("q0")
+        nc.vector.tensor_tensor(out=q0[:], in0=x_pos[:], in1=log_term[:], op=ALU.add)
+        w = column("w")
+        nc.vector.reciprocal(out=w[:], in_=z[:])
+        dr = small("dr")
+        nc.vector.tensor_reduce(out=dr[:], in_=drr[:], axis=AX.X, op=ALU.add)
+        q0_over_s = small("q0_over_s")
+        nc.vector.tensor_tensor(out=q0_over_s[:], in0=q0[:], in1=s_inv[:], op=ALU.mult)
+        sig_w_neg = small("sig_w_neg")
+        nc.scalar.activation(out=sig_w_neg[:], in_=sig_neg[:], func=ACT.Copy, scale=w[:])
+        gain = column("gain")
+        nc.scalar.activation(out=gain[:], in_=w[:], func=ACT.Square, scale=GAIN**0.5)
+        u_terms = small("u_terms")
+        u_mean = column("u_mean")
+        nc.vector.scalar_tensor_tensor(out=u_terms[:], in0=dr[:], scalar=w[:], in1=q0_over_s[:], op0=ALU.mult, op1=ALU.mult, accum_out=u_mean[:])
+        u = small("u")
+        nc.vector.tensor_tensor(out=u[:], in0=dr[:], in1=s_inv[:], op=ALU.mult)
+        y = small("y")
+        nc.vector.scalar_tensor_tensor(out=y[:], in0=u[:], scalar=u_mean[:], in1=sig[:], op0=ALU.subtract, op1=ALU.mult)
+        p_terms = small("p_terms")
+        p_neg = column("p_neg")
+        nc.vector.scalar_tensor_tensor(out=p_terms[:], in0=y[:], scalar=1.0, in1=sig_w_neg[:], op0=ALU.mult, op1=ALU.mult, accum_out=p_neg[:])
+        y_rest = small("y_rest")
+        nc.vector.tensor_tensor(out=y_rest[:], in0=y[:], in1=sig_rest[:], op=ALU.mult)
+        r_terms = small("r_terms")
+        r = column("r")
+        nc.scalar.activation(out=r_terms[:], in_=y[:], func=ACT.Square, accum_out=r[:])
+        t = small("t")
+        nc.vector.scalar_tensor_tensor(out=t[:], in0=y_rest[:], scalar=p_neg[:], in1=y[:], op0=ALU.add, op1=ALU.mult)
+        e = small("e")
+        nc.vector.scalar_tensor_tensor(out=e[:], in0=sig_w_neg[:], scalar=r[:], in1=t[:], op0=ALU.mult, op1=ALU.add)
+
+        half = PAGES // 2
+        for h, queue in enumerate((nc.scalar, nc.sync)):
+            pages = slice(h * half, (h + 1) * half)
+            res = sb.tile([P, half, PAGE], F32, name=f"res{h}")
+            nc.vector.scalar_tensor_tensor(
+                out=res[:], in0=e[:, pages].unsqueeze(2).to_broadcast([P, half, PAGE]), scalar=gain[:], in1=base_sb[:, pages], op0=ALU.mult, op1=ALU.add
+            )
+            queue.dma_start(out=out[:, h * half * PAGE : (h + 1) * half * PAGE], in_=res[:].rearrange("p g j -> p (g j)"))

@@ -32,59 +32,26 @@ def tile_attend_gppagequotas_kernel(tc, query, query2, keys_words, keys_scales, 
         ps = ctx.enter_context(tc.psum_pool(name="ps", bufs=1))
 
         offsets = sb.tile([P, SLOTS // 16], U16, name="offsets")
-        k_words = sb.tile([P, TOKENS], U16, name="k_words", align_bytes=64)
+        k_words = sb.tile([P, TOKENS], U16, name="k_words", tag="words", align_bytes=64)
         k_bytes = sb.tile([P, TOKENS], U8, name="k_bytes", align_bytes=64)
-        v_bytes = sb.tile([P, TOKENS], U8, name="v_bytes", align_bytes=64)
+        v_bytes = sb.tile([P, TOKENS], U8, name="v_bytes", tag="v_then_b", align_bytes=64)
         q_raw = sb.tile([P, PACK, ROWS], F32, name="q_raw")
-        q2_raw = sb.tile([P, PACK, ROWS], F32, name="q2_raw", tag="q2_then_v", align_bytes=64)
-        g_raw = sb.tile([P, PACK, ROWS], F32, name="g_raw", tag="g_then_pa")
-        base_sb = sb.tile([P, PAGES, PAGE], F32, name="base_sb")
+        q2_raw = sb.tile([P, PACK, ROWS], F32, name="q2_raw")
         reserve_sb = sb.tile([P, 1], F32, name="reserve_sb")
+        g_raw = sb.tile([P, PACK, ROWS], F32, name="g_raw", tag="g_then_pa")
 
-        def load_scale_rows(plane, rows):
-            by_place = rows[0].rearrange("(q r) c -> r q c", r=4)
-            for r in range(4):
-                nc.sync.dma_start(out=plane[r:P:32, :].bitcast(I32), in_=by_place[r].bitcast(I32))
+        def load_scale_rows(queues, plane, rows):
+            for q, queue in enumerate(queues):
+                queue.dma_start(out=plane[32 * q : 32 * q + 4, :].bitcast(I32), in_=rows[0, 4 * q : 4 * q + 4, :].bitcast(I32))
 
         def load_rows(queue, raw, src):
             queue.dma_start(out=raw[:], in_=src.rearrange("(p j) w -> p j w", j=PACK))
 
-        nc.vector.memset(k_bytes[:].bitcast(I32), 0)
-        nc.gpsimd.memset(v_bytes[:].bitcast(I32), 0)
-        nc.sync.dma_start(offsets[:], offs)
-        nc.scalar.dma_start(out=k_words[:].bitcast(I32), in_=keys_words[0].bitcast(I32))
-        load_rows(nc.scalar, q2_raw, query2)
-        load_scale_rows(k_bytes, keys_scales)
-        load_scale_rows(v_bytes, vals_scales)
-        load_rows(nc.gpsimd, q_raw, query)
-        load_rows(nc.gpsimd, g_raw, gout)
-        nc.gpsimd.dma_start(out=reserve_sb[:], in_=reserve)
-        nc.gpsimd.dma_start(out=base_sb[:].rearrange("p g j -> p (g j)"), in_=base)
+        def small(name):
+            return sb.tile([P, PAGES], F32, name=name)
 
-        kg_bytes = sb.tile([P, SLOTS], U8, name="kg_bytes", align_bytes=64)
-        kg_words = sb.tile([P, SLOTS], U16, name="kg_words", align_bytes=64)
-        vg_bytes = sb.tile([P, SLOTS], U8, name="vg_bytes", align_bytes=64)
-        vg_words = sb.tile([P, SLOTS], U16, name="vg_words", align_bytes=64)
-        qq_bf = sb.tile([P, 2, ROWS, PACK], BF16, name="qq_bf", align_bytes=64)
-        g_bf = sb.tile([P, ROWS, PACK], BF16, name="g_bf", align_bytes=64)
-        qq_codes = sb.tile([P, 2 * ROWS], U32, name="qq_codes", align_bytes=64)
-        qq_bytes = sb.tile([P, 2 * ROWS], U8, name="qq_bytes", align_bytes=64)
-        g_codes = sb.tile([P, ROWS], U32, name="g_codes", align_bytes=64)
-        g_bytes = sb.tile([P, ROWS], U8, name="g_bytes", align_bytes=64)
-
-        nc.scalar.copy(out=qq_bf[:, 0], in_=q2_raw[:].rearrange("p j w -> p w j"))
-        v_words = sb.tile([P, TOKENS], U16, name="v_words", tag="q2_then_v", align_bytes=64)
-        nc.sync.dma_start(out=v_words[:].bitcast(I32), in_=vals_words[0].bitcast(I32))
-        nc.scalar.copy(out=qq_bf[:, 1], in_=q_raw[:].rearrange("p j w -> p w j"))
-        nc.scalar.copy(out=g_bf[:], in_=g_raw[:].rearrange("p j w -> p w j"))
-
-        nc.vector.tensor_copy(kg_bytes[:], k_bytes[:].indirect(offsets[:]))
-        nc.vector.tensor_copy(kg_words[:], k_words[:].indirect(offsets[:]))
-        nc.vector.quantize_mx(out=qq_codes[:].bitcast(FP8X4), scales=qq_bytes[:], in_=qq_bf[:].rearrange("p s w j -> p (s w j)"))
-
-        b_ps = ps.tile([P, PAGES, PAGE], F32, name="b_ps")
-        a_ps = ps.tile([P, PAGES, PAGE], F32, name="a_ps")
-        c_ps = ps.tile([P, PAGES, PAGE], F32, name="c_ps")
+        def column(name):
+            return sb.tile([P, 1], F32, name=name)
 
         def product(acc, codes, scale_bytes, words, word_bytes):
             nc.tensor.matmul_mx(
@@ -97,18 +64,53 @@ def tile_attend_gppagequotas_kernel(tc, query, query2, keys_words, keys_scales, 
                 stop=True,
             )
 
-        product(b_ps, qq_codes[:, 0:ROWS], qq_bytes[:, 0:ROWS], kg_words, kg_bytes)
-        product(a_ps, qq_codes[:, ROWS:], qq_bytes[:, ROWS:], kg_words, kg_bytes)
+        nc.vector.memset(k_bytes[:].bitcast(I32), 0)
+        nc.vector.memset(v_bytes[:].bitcast(I32), 0)
+        nc.sync.dma_start(offsets[:], offs)
+        nc.scalar.dma_start(out=k_words[:].bitcast(I32), in_=keys_words[0].bitcast(I32))
+        load_rows(nc.scalar, q2_raw, query2)
+        load_rows(nc.gpsimd, q_raw, query)
+        load_rows(nc.gpsimd, g_raw, gout)
+        nc.gpsimd.dma_start(out=reserve_sb[:], in_=reserve)
+        load_scale_rows((nc.sync, nc.scalar, nc.sync, nc.scalar), k_bytes, keys_scales)
+        load_scale_rows((nc.sync,) * 4, v_bytes, vals_scales)
 
+        kg_bytes = sb.tile([P, SLOTS], U8, name="kg_bytes", align_bytes=64)
+        kg_words = sb.tile([P, SLOTS], U16, name="kg_words", tag="kg_then_base", align_bytes=64)
+        q2_bf = sb.tile([P, ROWS, PACK], BF16, name="q2_bf", align_bytes=64)
+        q_bf = sb.tile([P, ROWS, PACK], BF16, name="q_bf", align_bytes=64)
+        g_bf = sb.tile([P, ROWS, PACK], BF16, name="g_bf", align_bytes=64)
+        q2_codes = sb.tile([P, ROWS], U32, name="q2_codes", align_bytes=64)
+        q2_bytes = sb.tile([P, ROWS], U8, name="q2_bytes", align_bytes=64)
+        q_codes = sb.tile([P, ROWS], U32, name="q_codes", align_bytes=64)
+        q_bytes = sb.tile([P, ROWS], U8, name="q_bytes", align_bytes=64)
+        g_codes = sb.tile([P, ROWS], U32, name="g_codes", align_bytes=64)
+        g_bytes = sb.tile([P, ROWS], U8, name="g_bytes", align_bytes=64)
+
+        nc.scalar.copy(out=q2_bf[:], in_=q2_raw[:].rearrange("p j w -> p w j"))
+        nc.scalar.copy(out=q_bf[:], in_=q_raw[:].rearrange("p j w -> p w j"))
+        nc.scalar.copy(out=g_bf[:], in_=g_raw[:].rearrange("p j w -> p w j"))
+        nc.vector.tensor_copy(kg_words[:], k_words[:].indirect(offsets[:]))
+        v_words = sb.tile([P, TOKENS], U16, name="v_words", tag="words", align_bytes=64)
+        nc.sync.dma_start(out=v_words[:].bitcast(I32), in_=vals_words[0].bitcast(I32))
+        nc.vector.quantize_mx(out=q2_codes[:].bitcast(FP8X4), scales=q2_bytes[:], in_=q2_bf[:].rearrange("p w j -> p (w j)"))
+        nc.vector.tensor_copy(kg_bytes[:], k_bytes[:].indirect(offsets[:]))
+        nc.vector.quantize_mx(out=q_codes[:].bitcast(FP8X4), scales=q_bytes[:], in_=q_bf[:].rearrange("p w j -> p (w j)"))
+
+        b_ps = ps.tile([P, PAGES, PAGE], F32, name="b_ps")
+        a_ps = ps.tile([P, PAGES, PAGE], F32, name="a_ps")
+        c_ps = ps.tile([P, PAGES, PAGE], F32, name="c_ps")
+        product(b_ps, q2_codes[:], q2_bytes[:], kg_words, kg_bytes)
+        product(a_ps, q_codes[:], q_bytes[:], kg_words, kg_bytes)
+
+        base_sb = sb.tile([P, PAGES, PAGE], F32, name="base_sb", tag="kg_then_base", align_bytes=64)
+        nc.sync.dma_start(out=base_sb[:].rearrange("p g j -> p (g j)"), in_=base)
+
+        vg_bytes = sb.tile([P, SLOTS], U8, name="vg_bytes", align_bytes=64)
+        vg_words = sb.tile([P, SLOTS], U16, name="vg_words", align_bytes=64)
         nc.vector.tensor_copy(vg_bytes[:], v_bytes[:].indirect(offsets[:]))
-
-        def small(name):
-            return sb.tile([P, PAGES], F32, name=name)
-
-        def column(name):
-            return sb.tile([P, 1], F32, name=name)
-
-        b_sum = small("b_sum")
+        nc.vector.quantize_mx(out=g_codes[:].bitcast(FP8X4), scales=g_bytes[:], in_=g_bf[:].rearrange("p w j -> p (w j)"))
+        b_sum = sb.tile([P, PAGES], F32, name="b_sum", tag="v_then_b", align_bytes=64)
         nc.vector.tensor_reduce(out=b_sum[:], in_=b_ps[:], axis=AX.X, op=ALU.add)
 
         pa = sb.tile([P, PAGES, PAGE], F32, name="pa", tag="g_then_pa")
@@ -137,30 +139,34 @@ def tile_attend_gppagequotas_kernel(tc, query, query2, keys_words, keys_scales, 
         nc.scalar.activation(out=sig_rest[:], in_=half_tanh[:], func=ACT.Copy, scale=-0.5, bias=0.5)
 
         nc.vector.tensor_copy(vg_words[:], v_words[:].indirect(offsets[:]))
-        nc.vector.quantize_mx(out=g_codes[:].bitcast(FP8X4), scales=g_bytes[:], in_=g_bf[:].rearrange("p w j -> p (w j)"))
         product(c_ps, g_codes[:], g_bytes[:], vg_words, vg_bytes)
 
-        s = small("s")
-        nc.vector.tensor_reduce(out=s[:], in_=pa[:], axis=AX.X, op=ALU.add)
+        s_q0 = sb.tile([P, 3, PAGES], F32, name="s_q0", tag="words", align_bytes=64)
+        s = s_q0[:, 0]
+        q0 = s_q0[:, 1]
+        nc.vector.tensor_reduce(out=s, in_=pa[:], axis=AX.X, op=ALU.add)
         s_inv = small("s_inv")
-        nc.vector.reciprocal(out=s_inv[:], in_=s[:])
-        drr = sb.tile([P, PAGES, PAGE], F32, name="drr")
-        nc.vector.tensor_tensor(out=drr[:], in0=c_ps[:], in1=pa[:], op=ALU.mult)
-        q0 = small("q0")
-        nc.vector.tensor_tensor(out=q0[:], in0=x_pos[:], in1=log_term[:], op=ALU.add)
-        w = column("w")
-        nc.vector.reciprocal(out=w[:], in_=z[:])
+        nc.vector.reciprocal(out=s_inv[:], in_=s)
+        half = PAGES // 2
+        halves = (slice(0, half), slice(half, PAGES))
+        drr = [sb.tile([P, half, PAGE], F32, name=f"drr{h}") for h in range(2)]
         dr = small("dr")
-        nc.vector.tensor_reduce(out=dr[:], in_=drr[:], axis=AX.X, op=ALU.add)
+        nc.vector.tensor_tensor(out=drr[0][:], in0=c_ps[:, halves[0]], in1=pa[:, halves[0]], op=ALU.mult)
+        nc.vector.tensor_tensor(out=q0, in0=x_pos[:], in1=log_term[:], op=ALU.add)
+        nc.vector.tensor_tensor(out=drr[1][:], in0=c_ps[:, halves[1]], in1=pa[:, halves[1]], op=ALU.mult)
+        w = s_q0[:, 2, 0:1]
+        nc.vector.reciprocal(out=w, in_=z[:])
+        nc.vector.tensor_reduce(out=dr[:, halves[0]], in_=drr[0][:], axis=AX.X, op=ALU.add)
         q0_over_s = small("q0_over_s")
-        nc.vector.tensor_tensor(out=q0_over_s[:], in0=q0[:], in1=s_inv[:], op=ALU.mult)
+        nc.vector.tensor_tensor(out=q0_over_s[:], in0=q0, in1=s_inv[:], op=ALU.mult)
+        nc.vector.tensor_reduce(out=dr[:, halves[1]], in_=drr[1][:], axis=AX.X, op=ALU.add)
         sig_w_neg = small("sig_w_neg")
-        nc.scalar.activation(out=sig_w_neg[:], in_=sig_neg[:], func=ACT.Copy, scale=w[:])
+        nc.scalar.activation(out=sig_w_neg[:], in_=sig_neg[:], func=ACT.Copy, scale=w)
         gain = column("gain")
-        nc.scalar.activation(out=gain[:], in_=w[:], func=ACT.Square, scale=GAIN**0.5)
+        nc.scalar.activation(out=gain[:], in_=w, func=ACT.Square, scale=GAIN**0.5)
         u_terms = small("u_terms")
         u_mean = column("u_mean")
-        nc.vector.scalar_tensor_tensor(out=u_terms[:], in0=dr[:], scalar=w[:], in1=q0_over_s[:], op0=ALU.mult, op1=ALU.mult, accum_out=u_mean[:])
+        nc.vector.scalar_tensor_tensor(out=u_terms[:], in0=dr[:], scalar=w, in1=q0_over_s[:], op0=ALU.mult, op1=ALU.mult, accum_out=u_mean[:])
         u = small("u")
         nc.vector.tensor_tensor(out=u[:], in0=dr[:], in1=s_inv[:], op=ALU.mult)
         y = small("y")
@@ -178,7 +184,6 @@ def tile_attend_gppagequotas_kernel(tc, query, query2, keys_words, keys_scales, 
         e = small("e")
         nc.vector.scalar_tensor_tensor(out=e[:], in0=sig_w_neg[:], scalar=r[:], in1=t[:], op0=ALU.mult, op1=ALU.add)
 
-        half = PAGES // 2
         for h, queue in enumerate((nc.scalar, nc.sync)):
             pages = slice(h * half, (h + 1) * half)
             res = sb.tile([P, half, PAGE], F32, name=f"res{h}")

@@ -113,8 +113,14 @@ def tile_attend_gppagequotas_kernel(tc, query, query2, keys_words, keys_scales, 
         b_sum = sb.tile([P, PAGES], F32, name="b_sum", tag="v_then_b", align_bytes=64)
         nc.vector.tensor_reduce(out=b_sum[:], in_=b_ps[:], axis=AX.X, op=ALU.add)
 
-        pa = sb.tile([P, PAGES, PAGE], F32, name="pa", tag="g_then_pa")
-        nc.scalar.activation(out=pa[:], in_=a_ps[:], func=ACT.Exp)
+        half = PAGES // 2
+        halves = (slice(0, half), slice(half, PAGES))
+        pa = [
+            sb.tile([P, half, PAGE], F32, name="pa0", tag="g_then_pa"),
+            sb.tile([P, half, PAGE], F32, name="pa1"),
+        ]
+        for h in range(2):
+            nc.scalar.activation(out=pa[h][:], in_=a_ps[:, halves[h]], func=ACT.Exp)
         x_abs = small("x_abs")
         nc.scalar.activation(out=x_abs[:], in_=b_sum[:], func=ACT.Abs, scale=3.0 / PAGE)
         x_pos = small("x_pos")
@@ -138,26 +144,30 @@ def tile_attend_gppagequotas_kernel(tc, query, query2, keys_words, keys_scales, 
         sig_rest = small("sig_rest")
         nc.scalar.activation(out=sig_rest[:], in_=half_tanh[:], func=ACT.Copy, scale=-0.5, bias=0.5)
 
+        fold4 = sb.tile([P, PAGES, 4], F32, name="fold4")
+        for h in range(2):
+            nc.gpsimd.tensor_tensor(out=fold4[:, halves[h]], in0=pa[h][:, :, 0:4], in1=pa[h][:, :, 4:8], op=ALU.add)
+        fold2 = sb.tile([P, PAGES, 2], F32, name="fold2")
+        nc.gpsimd.tensor_tensor(out=fold2[:], in0=fold4[:, :, 0:2], in1=fold4[:, :, 2:4], op=ALU.add)
+        s = small("s")
+        nc.gpsimd.tensor_tensor(out=s[:], in0=fold2[:, :, 0], in1=fold2[:, :, 1], op=ALU.add)
+
         nc.vector.tensor_copy(vg_words[:], v_words[:].indirect(offsets[:]))
         product(c_ps, g_codes[:], g_bytes[:], vg_words, vg_bytes)
 
-        s_q0 = sb.tile([P, 3, PAGES], F32, name="s_q0", tag="words", align_bytes=64)
-        s = s_q0[:, 0]
-        q0 = s_q0[:, 1]
-        nc.vector.tensor_reduce(out=s, in_=pa[:], axis=AX.X, op=ALU.add)
-        s_inv = small("s_inv")
-        nc.vector.reciprocal(out=s_inv[:], in_=s)
-        half = PAGES // 2
-        halves = (slice(0, half), slice(half, PAGES))
+        s_inv = sb.tile([P, PAGES], F32, name="s_inv", tag="words", align_bytes=64)
+        nc.vector.reciprocal(out=s_inv[:], in_=s[:])
         drr = [sb.tile([P, half, PAGE], F32, name=f"drr{h}") for h in range(2)]
-        dr = small("dr")
-        nc.vector.tensor_tensor(out=drr[0][:], in0=c_ps[:, halves[0]], in1=pa[:, halves[0]], op=ALU.mult)
+        for h in range(2):
+            nc.vector.tensor_tensor(out=drr[h][:], in0=c_ps[:, halves[h]], in1=pa[h][:], op=ALU.mult)
+        quota = sb.tile([P, 2, PAGES], F32, name="quota", tag="g_then_pa")
+        q0 = quota[:, 0]
+        w = quota[:, 1, 0:1]
         nc.vector.tensor_tensor(out=q0, in0=x_pos[:], in1=log_term[:], op=ALU.add)
-        nc.vector.tensor_tensor(out=drr[1][:], in0=c_ps[:, halves[1]], in1=pa[:, halves[1]], op=ALU.mult)
-        w = s_q0[:, 2, 0:1]
         nc.vector.reciprocal(out=w, in_=z[:])
-        nc.vector.tensor_reduce(out=dr[:, halves[0]], in_=drr[0][:], axis=AX.X, op=ALU.add)
+        dr = small("dr")
         q0_over_s = small("q0_over_s")
+        nc.vector.tensor_reduce(out=dr[:, halves[0]], in_=drr[0][:], axis=AX.X, op=ALU.add)
         nc.vector.tensor_tensor(out=q0_over_s[:], in0=q0, in1=s_inv[:], op=ALU.mult)
         nc.vector.tensor_reduce(out=dr[:, halves[1]], in_=drr[1][:], axis=AX.X, op=ALU.add)
         sig_w_neg = small("sig_w_neg")

from contextlib import ExitStack

import concourse.mybir as mybir

F32 = mybir.dt.float32
BF16 = mybir.dt.bfloat16
I32 = mybir.dt.int32
U32 = mybir.dt.uint32
U16 = mybir.dt.uint16
U8 = mybir.dt.uint8
FP8X4 = mybir.dt.float8_e4m3fn_x4
FP4X4 = mybir.dt.float4_e2m1fn_x4
ALU = mybir.AluOpType
ACT = mybir.ActivationFunctionType
AX = mybir.AxisListType

P = 128
PACK = 4
TOKENS = 2048
SLOTS = 512
ROWS = 128
PAGES = 64
PAGE = 8
FLOPS = 3 * 2 * 512 * ROWS * SLOTS
GAIN = 9.0 * 3.0 * 1024.0 * 2.0 * 1024.0 / 64.0


def tile_attend_gppagequotas_kernel(tc, query, query2, keys_words, keys_scales, reserve, gout, vals_words, vals_scales, base, offs, out):
    nc = tc.nc
    with ExitStack() as ctx:
        sb = ctx.enter_context(tc.tile_pool(name="sb", bufs=1))
        ps = ctx.enter_context(tc.psum_pool(name="ps", bufs=1))

        offsets = sb.tile([P, SLOTS // 16], U16, name="offsets")
        k_words = sb.tile([P, TOKENS], U16, name="k_words", tag="words", align_bytes=64)
        k_bytes = sb.tile([P, TOKENS], U8, name="k_bytes", align_bytes=64)
        v_bytes = sb.tile([P, TOKENS], U8, name="v_bytes", tag="v_then_b", align_bytes=64)
        q_raw = sb.tile([P, PACK, ROWS], F32, name="q_raw")
        q2_raw = sb.tile([P, PACK, ROWS], F32, name="q2_raw")
        reserve_sb = sb.tile([P, 1], F32, name="reserve_sb")
        g_raw = sb.tile([P, PACK, ROWS], F32, name="g_raw", tag="g_then_pa")

        def load_scale_rows(queues, plane, rows):
            for q, queue in enumerate(queues):
                queue.dma_start(out=plane[32 * q : 32 * q + 4, :].bitcast(I32), in_=rows[0, 4 * q : 4 * q + 4, :].bitcast(I32))

        def load_rows(queue, raw, src):
            queue.dma_start(out=raw[:], in_=src.rearrange("(p j) w -> p j w", j=PACK))

        def small(name):
            return sb.tile([P, PAGES], F32, name=name)

        def column(name):
            return sb.tile([P, 1], F32, name=name)

        def product(acc, codes, scale_bytes, words, word_bytes):
            nc.tensor.matmul_mx(
                out=acc[:].rearrange("p g j -> p (g j)"),
                lhsT=codes.bitcast(FP8X4),
                lhsT_scale=scale_bytes,
                rhs=words[:].bitcast(FP4X4),
                rhs_scale=word_bytes[:],
                start=True,
                stop=True,
            )

        nc.vector.memset(k_bytes[:].bitcast(I32), 0)
        nc.vector.memset(v_bytes[:].bitcast(I32), 0)
        nc.sync.dma_start(offsets[:], offs)
        nc.scalar.dma_start(out=k_words[:].bitcast(I32), in_=keys_words[0].bitcast(I32))
        load_rows(nc.scalar, q2_raw, query2)
        load_rows(nc.gpsimd, q_raw, query)
        load_rows(nc.gpsimd, g_raw, gout)
        nc.gpsimd.dma_start(out=reserve_sb[:], in_=reserve)
        load_scale_rows((nc.sync, nc.scalar, nc.sync, nc.scalar), k_bytes, keys_scales)
        load_scale_rows((nc.sync,) * 4, v_bytes, vals_scales)

        kg_bytes = sb.tile([P, SLOTS], U8, name="kg_bytes", align_bytes=64)
        kg_words = sb.tile([P, SLOTS], U16, name="kg_words", tag="kg_then_base", align_bytes=64)
        q2_bf = sb.tile([P, ROWS, PACK], BF16, name="q2_bf", align_bytes=64)
        q_bf = sb.tile([P, ROWS, PACK], BF16, name="q_bf", align_bytes=64)
        g_bf = sb.tile([P, ROWS, PACK], BF16, name="g_bf", align_bytes=64)
        q2_codes = sb.tile([P, ROWS], U32, name="q2_codes", align_bytes=64)
        q2_bytes = sb.tile([P, ROWS], U8, name="q2_bytes", align_bytes=64)
        q_codes = sb.tile([P, ROWS], U32, name="q_codes", align_bytes=64)
        q_bytes = sb.tile([P, ROWS], U8, name="q_bytes", align_bytes=64)
        g_codes = sb.tile([P, ROWS], U32, name="g_codes", align_bytes=64)
        g_bytes = sb.tile([P, ROWS], U8, name="g_bytes", align_bytes=64)

        nc.scalar.copy(out=q2_bf[:], in_=q2_raw[:].rearrange("p j w -> p w j"))
        nc.scalar.copy(out=q_bf[:], in_=q_raw[:].rearrange("p j w -> p w j"))
        nc.scalar.copy(out=g_bf[:], in_=g_raw[:].rearrange("p j w -> p w j"))
        nc.vector.tensor_copy(kg_words[:], k_words[:].indirect(offsets[:]))
        v_words = sb.tile([P, TOKENS], U16, name="v_words", tag="words", align_bytes=64)
        nc.sync.dma_start(out=v_words[:].bitcast(I32), in_=vals_words[0].bitcast(I32))
        nc.vector.quantize_mx(out=q2_codes[:].bitcast(FP8X4), scales=q2_bytes[:], in_=q2_bf[:].rearrange("p w j -> p (w j)"))
        nc.vector.tensor_copy(kg_bytes[:], k_bytes[:].indirect(offsets[:]))
        nc.vector.quantize_mx(out=q_codes[:].bitcast(FP8X4), scales=q_bytes[:], in_=q_bf[:].rearrange("p w j -> p (w j)"))

        b_ps = ps.tile([P, PAGES, PAGE], F32, name="b_ps")
        a_ps = ps.tile([P, PAGES, PAGE], F32, name="a_ps")
        c_ps = ps.tile([P, PAGES, PAGE], F32, name="c_ps")
        product(b_ps, q2_codes[:], q2_bytes[:], kg_words, kg_bytes)
        product(a_ps, q_codes[:], q_bytes[:], kg_words, kg_bytes)

        base_sb = sb.tile([P, PAGES, PAGE], F32, name="base_sb", tag="kg_then_base", align_bytes=64)
        nc.sync.dma_start(out=base_sb[:].rearrange("p g j -> p (g j)"), in_=base)

        vg_bytes = sb.tile([P, SLOTS], U8, name="vg_bytes", align_bytes=64)
        vg_words = sb.tile([P, SLOTS], U16, name="vg_words", align_bytes=64)
        nc.vector.tensor_copy(vg_bytes[:], v_bytes[:].indirect(offsets[:]))
        nc.vector.quantize_mx(out=g_codes[:].bitcast(FP8X4), scales=g_bytes[:], in_=g_bf[:].rearrange("p w j -> p (w j)"))
        b_sum = sb.tile([P, PAGES], F32, name="b_sum", tag="v_then_b", align_bytes=64)
        nc.vector.tensor_reduce(out=b_sum[:], in_=b_ps[:], axis=AX.X, op=ALU.add)

        half = PAGES // 2
        halves = (slice(0, half), slice(half, PAGES))
        pa = [
            sb.tile([P, half, PAGE], F32, name="pa0", tag="g_then_pa"),
            sb.tile([P, half, PAGE], F32, name="pa1"),
        ]
        for h in range(2):
            nc.scalar.activation(out=pa[h][:], in_=a_ps[:, halves[h]], func=ACT.Exp)
        x_abs = small("x_abs")
        nc.scalar.activation(out=x_abs[:], in_=b_sum[:], func=ACT.Abs, scale=3.0 / PAGE)
        x_pos = small("x_pos")
        x_pos_sum = column("x_pos_sum")
        nc.scalar.activation(out=x_pos[:], in_=b_sum[:], func=ACT.Relu, scale=3.0 / PAGE, accum_out=x_pos_sum[:])
        half_tanh = small("half_tanh")
        nc.scalar.activation(out=half_tanh[:], in_=b_sum[:], func=ACT.Tanh, scale=1.5 / PAGE)
        decay = small("decay")
        nc.scalar.activation(out=decay[:], in_=x_abs[:], func=ACT.Exp, scale=-1.0)
        log_term = small("log_term")
        log_sum = column("log_sum")
        nc.scalar.activation(out=log_term[:], in_=decay[:], func=ACT.Ln, bias=1.0, accum_out=log_sum[:])
        z_part = column("z_part")
        nc.scalar.activation(out=z_part[:], in_=x_pos_sum[:], func=ACT.Identity, bias=reserve_sb[:])
        z = column("z")
        nc.scalar.activation(out=z[:], in_=log_sum[:], func=ACT.Identity, bias=z_part[:])
        sig = small("sig")
        nc.scalar.activation(out=sig[:], in_=half_tanh[:], func=ACT.Copy, scale=0.5, bias=0.5)
        sig_neg = small("sig_neg")
        nc.scalar.activation(out=sig_neg[:], in_=half_tanh[:], func=ACT.Copy, scale=-0.5, bias=-0.5)
        sig_rest = small("sig_rest")
        nc.scalar.activation(out=sig_rest[:], in_=half_tanh[:], func=ACT.Copy, scale=-0.5, bias=0.5)

        fold4 = sb.tile([P, PAGES, 4], F32, name="fold4")
        for h in range(2):
            nc.gpsimd.tensor_tensor(out=fold4[:, halves[h]], in0=pa[h][:, :, 0:4], in1=pa[h][:, :, 4:8], op=ALU.add)
        fold2 = sb.tile([P, PAGES, 2], F32, name="fold2")
        nc.gpsimd.tensor_tensor(out=fold2[:], in0=fold4[:, :, 0:2], in1=fold4[:, :, 2:4], op=ALU.add)
        s = small("s")
        nc.gpsimd.tensor_tensor(out=s[:], in0=fold2[:, :, 0], in1=fold2[:, :, 1], op=ALU.add)

        nc.vector.tensor_copy(vg_words[:], v_words[:].indirect(offsets[:]))
        product(c_ps, g_codes[:], g_bytes[:], vg_words, vg_bytes)

        s_inv = sb.tile([P, PAGES], F32, name="s_inv", tag="words", align_bytes=64)
        nc.vector.reciprocal(out=s_inv[:], in_=s[:])
        drr = [sb.tile([P, half, PAGE], F32, name=f"drr{h}") for h in range(2)]
        for h in range(2):
            nc.vector.tensor_tensor(out=drr[h][:], in0=c_ps[:, halves[h]], in1=pa[h][:], op=ALU.mult)
        quota = sb.tile([P, 2, PAGES], F32, name="quota", tag="g_then_pa")
        q0 = quota[:, 0]
        w = quota[:, 1, 0:1]
        nc.vector.tensor_tensor(out=q0, in0=x_pos[:], in1=log_term[:], op=ALU.add)
        nc.vector.reciprocal(out=w, in_=z[:])
        dr = small("dr")
        q0_over_s = small("q0_over_s")
        nc.vector.tensor_reduce(out=dr[:, halves[0]], in_=drr[0][:], axis=AX.X, op=ALU.add)
        nc.vector.tensor_tensor(out=q0_over_s[:], in0=q0, in1=s_inv[:], op=ALU.mult)
        nc.vector.tensor_reduce(out=dr[:, halves[1]], in_=drr[1][:], axis=AX.X, op=ALU.add)
        sig_w_neg = small("sig_w_neg")
        nc.scalar.activation(out=sig_w_neg[:], in_=sig_neg[:], func=ACT.Copy, scale=w)
        gain = column("gain")
        nc.scalar.activation(out=gain[:], in_=w, func=ACT.Square, scale=GAIN**0.5)
        u_terms = small("u_terms")
        u_mean = column("u_mean")
        nc.vector.scalar_tensor_tensor(out=u_terms[:], in0=dr[:], scalar=w, in1=q0_over_s[:], op0=ALU.mult, op1=ALU.mult, accum_out=u_mean[:])
        u = small("u")
        nc.vector.tensor_tensor(out=u[:], in0=dr[:], in1=s_inv[:], op=ALU.mult)
        y = small("y")
        nc.vector.scalar_tensor_tensor(out=y[:], in0=u[:], scalar=u_mean[:], in1=sig[:], op0=ALU.subtract, op1=ALU.mult)
        p_terms = small("p_terms")
        p_neg = column("p_neg")
        nc.vector.scalar_tensor_tensor(out=p_terms[:], in0=y[:], scalar=1.0, in1=sig_w_neg[:], op0=ALU.mult, op1=ALU.mult, accum_out=p_neg[:])
        y_rest = small("y_rest")
        nc.vector.tensor_tensor(out=y_rest[:], in0=y[:], in1=sig_rest[:], op=ALU.mult)
        r_terms = small("r_terms")
        r = column("r")
        nc.scalar.activation(out=r_terms[:], in_=y[:], func=ACT.Square, accum_out=r[:])
        t = small("t")
        nc.vector.scalar_tensor_tensor(out=t[:], in0=y_rest[:], scalar=p_neg[:], in1=y[:], op0=ALU.add, op1=ALU.mult)
        e = small("e")
        nc.vector.scalar_tensor_tensor(out=e[:], in0=sig_w_neg[:], scalar=r[:], in1=t[:], op0=ALU.mult, op1=ALU.add)

        for h, queue in enumerate((nc.scalar, nc.sync)):
            pages = slice(h * half, (h + 1) * half)
            res = sb.tile([P, half, PAGE], F32, name=f"res{h}")
            nc.vector.scalar_tensor_tensor(
                out=res[:], in0=e[:, pages].unsqueeze(2).to_broadcast([P, half, PAGE]), scalar=gain[:], in1=base_sb[:, pages], op0=ALU.mult, op1=ALU.add
            )
            queue.dma_start(out=out[:, h * half * PAGE : (h + 1) * half * PAGE], in_=res[:].rearrange("p g j -> p (g j)"))
